import numpy as np
import ml_dtypes


def mxq(x, axis, fmt="e4m3"):
    dtype, down = {"e4m3": (ml_dtypes.float8_e4m3fn, 7), "e5m2": (ml_dtypes.float8_e5m2, 14)}[fmt]
    v = np.moveaxis(np.asarray(x, np.float32).astype(ml_dtypes.bfloat16).astype(np.float64), axis, -1)
    blocks = v.reshape(v.shape[:-1] + (-1, 32))
    amax = np.abs(blocks).max(-1, keepdims=True)
    byte = np.maximum(np.where(amax > 0, np.frexp(amax)[1] - 1 + 127, 0) - down, 1)
    scale = np.exp2(byte - 127.0)
    codes = (blocks / scale).astype(np.float32).astype(dtype).astype(np.float64)
    return np.moveaxis((codes * scale).reshape(v.shape), -1, axis)


WIDE = False


def mx_kscale(k):
    if not WIDE:
        return np.ones(k)
    levels = np.array([10, -10, 5, -5, 0])
    if k % 512:
        return np.exp2(np.random.permutation(np.resize(levels, k // 32))).repeat(32)
    a = np.empty((k // 512, 16))
    for p in range(k // 512):
        a[p, :8] = np.random.permutation(np.resize(levels, 8))
        for g in range(8):
            far = levels[np.abs(levels - a[p, g]) >= 10]
            a[p, g + 8] = far[np.random.randint(len(far))]
    return np.exp2(a.ravel()).repeat(32)


def f64(x):
    return np.asarray(x).astype(np.float64)


def striped(idx):
    return np.tile(idx.reshape(-1, 16).T, (8, 1)).astype(np.uint16)


def unstriped(offs):
    return offs[:16].T.reshape(-1).astype(np.int64)


E2M1 = np.array([0.0, 0.5, 1.0, 1.5, 2.0, 3.0, 4.0, 6.0, -0.0, -0.5, -1.0, -1.5, -2.0, -3.0, -4.0, -6.0])


def pack_weight(w, fmt):
    k, n = w.shape
    w = f64(np.asarray(w, np.float32).astype(ml_dtypes.bfloat16)).reshape(k // 32, 32, n)
    amax = np.abs(w).max(1)
    if fmt == "e4m3":
        byte = np.frexp(amax)[1] - 1 + 127 - 7
    else:
        mant, ex = np.frexp(amax / 6.0)
        byte = np.where(mant > 0.5, ex, ex - 1) + 127
    byte = np.clip(np.where(amax > 0, byte, 1), 1, 254)
    scaled = (w * np.exp2(127.0 - byte)[:, None, :]).reshape(k, n).astype(np.float32)
    by_word = np.ascontiguousarray(scaled.reshape(k // 512, 128, 4, n).transpose(0, 1, 3, 2))
    if fmt == "e4m3":
        words = by_word.astype(ml_dtypes.float8_e4m3fn).view(np.uint8)
    else:
        c = by_word.astype(ml_dtypes.float4_e2m1fn).view(np.uint8) & 0xF
        words = (c[..., 0::2] | (c[..., 1::2] << 4)).reshape(k // 512, 128, 2 * n)
    return np.ascontiguousarray(words), np.ascontiguousarray(byte.astype(np.uint8).reshape(k // 512, 16, n))


def unpack_weight(words, scales, fmt):
    g, _, n = scales.shape
    words = np.ascontiguousarray(words).reshape(g, 128, n, -1)
    if fmt == "e4m3":
        vals = words.view(ml_dtypes.float8_e4m3fn).astype(np.float64)
    else:
        nib = np.empty((g, 128, n, 4), np.uint8)
        nib[..., 0::2] = words & 0xF
        nib[..., 1::2] = words >> 4
        vals = E2M1[nib]
    vals = vals * np.repeat(np.exp2(scales.astype(np.float64) - 127.0), 8, axis=1)[..., None]
    return vals.transpose(0, 1, 3, 2).reshape(g * 512, n)


def gelu(v):
    return 0.5 * v * (1.0 + np.tanh(np.sqrt(2.0 / np.pi) * (v + 0.044715 * v**3)))


K, K1, H, T, S, S2, T3, P = 1024, 512, 1024, 4096, 1024, 512, 2048, 512

def setup_inputs():
    n = np.random.standard_normal
    s = mx_kscale(K)[:, None]
    u = mx_kscale(H)[:, None]
    tab_words, tab_scales = pack_weight(n((K, T)) * s, "e4m3")
    w4_words, w4_scales = pack_weight(1.5 * n((K - K1, H)) / np.sqrt(K) / s[K1:], "e2m1")
    tab2_words, tab2_scales = pack_weight(n((H, T3)) / np.sqrt(H) / u, "e4m3")
    return {
        "tab_words": tab_words, "tab_scales": tab_scales,
        "offs": striped(np.random.permutation(T)[:S]),
        "w1": (1.5 * n((K1, H)) / np.sqrt(K) / s[:K1]).astype(np.float32),
        "w4_words": w4_words, "w4_scales": w4_scales,
        "b": (0.6 * n(H)).astype(np.float32),
        "gain": (np.exp(0.3 * n(H)) * u[:, 0]).astype(np.float32),
        "tried": np.exp(0.4 * n(H)).astype(np.float32),
        "tab2_words": tab2_words, "tab2_scales": tab2_scales,
        "offs2": striped(np.random.permutation(T3)[:S2]),
        "pos1": striped(np.random.permutation(S)[:P]),
        "pos2": striped(np.random.permutation(S)[:P]),
        "veil": np.exp(0.4 * n(S2)).astype(np.float32),
    }

def reference(tab_words, tab_scales, offs, w1, w4_words, w4_scales, b, gain, tried,
              tab2_words, tab2_scales, offs2, pos1, pos2, veil):
    v = unpack_weight(tab_words, tab_scales, "e4m3")[:, unstriped(offs)]
    w4 = unpack_weight(w4_words, w4_scales, "e2m1")
    w1q = mxq(f64(w1), 0, "e4m3")
    d = (w1q.T @ v[:K1] + w4.T @ v[K1:]) + f64(b)[:, None]
    h = f64(gain)[:, None] * (d / (1.0 + np.exp(-d)))
    x1 = mxq(f64(tried)[:, None] * h[:, unstriped(pos1)], 0, "e4m3")
    x2 = mxq(h[:, unstriped(pos2)], 0, "e4m3")
    v2 = unpack_weight(tab2_words, tab2_scales, "e4m3")[:, unstriped(offs2)]
    e = v2.T @ x1 + v2.T @ x2
    return f64(veil)[:, None] * e

@@ -1,0 +1,244 @@
+from contextlib import ExitStack
+
+import concourse.mybir as mybir
+
+K, K1, H, T, S, S2, T3, NP = 1024, 512, 1024, 4096, 1024, 512, 2048, 512
+FLOPS = 2 * K * H * S + 2 * 2 * H * S2 * NP
+
+F32 = mybir.dt.float32
+BF16 = mybir.dt.bfloat16
+I32 = mybir.dt.int32
+U32 = mybir.dt.uint32
+U16 = mybir.dt.uint16
+U8 = mybir.dt.uint8
+FP8X4 = mybir.dt.float8_e4m3fn_x4
+FP4X4 = mybir.dt.float4_e2m1fn_x4
+ACT = mybir.ActivationFunctionType
+ALU = mybir.AluOpType
+
+P = 128
+BANK = 512
+
+
+def tile_list_gown_veil_suggestion_kernel(
+    tc, tab_words, tab_scales, offs, w1, w4_words, w4_scales, b, gain, tried,
+    tab2_words, tab2_scales, offs2, pos1, pos2, veil, out,
+):
+    nc = tc.nc
+    with ExitStack() as ctx:
+        keep = ctx.enter_context(tc.tile_pool(name="keep", bufs=1))
+        psum = ctx.enter_context(tc.psum_pool(name="psum", bufs=8))
+
+        def tile(name, shape, dtype, tag=None):
+            return keep.tile(shape, dtype, name=name, tag=tag or name, align_bytes=64)
+
+        def words_of(table, a):
+            return table[a].rearrange("p t i -> p (t i)").bitcast(I32)
+
+        idx = tile("idx", [P, S // 16], U16)
+        idx2 = tile("idx2", [P, S2 // 16], U16)
+        p1 = tile("p1", [P, NP // 16], U16)
+        p2 = tile("p2", [P, NP // 16], U16)
+        tabw = [tile("tabw%d" % a, [P, T], I32) for a in range(2)]
+        tabs = tile("tabs", [P, T], U8)
+        tab2w = [tile("tab2w%d" % a, [P, T3], I32) for a in range(2)]
+        tab2s = tile("tab2s", [P, T3], U8)
+        w4raw = tile("w4raw", [P, 2 * H], U8)
+        w4sraw = tile("w4sraw", [P, H], U8)
+        w1raw = [tile("w1raw%d" % g, [P, 4, 512], F32) for g in range(2)]
+        bias = tile("bias", [P, 2, 4], F32)
+        gn = tile("gn", [P, 2, 4], F32)
+        tr = tile("tr", [P, 2, 4], F32)
+        vl = tile("vl", [P, 4], F32)
+
+        nc.vector.memset(w4sraw[:].bitcast(I32), 0)
+        nc.vector.memset(tabs[:].bitcast(I32), 0)
+        nc.vector.memset(tab2s[:].bitcast(I32), 0)
+
+        def load_w1(g):
+            nc.sync.dma_start(out=w1raw[g][:], in_=w1[:, 512 * g : 512 * g + 512].rearrange("(p j) c -> p j c", j=4))
+
+        nc.sync.dma_start(idx[:], offs)
+        nc.sync.dma_start(out=w4raw[:].bitcast(I32), in_=w4_words[0].bitcast(I32))
+        for q in range(4):
+            nc.sync.dma_start(out=w4sraw[32 * q : 32 * q + 4, :].bitcast(I32), in_=w4_scales[0, 4 * q : 4 * q + 4, :].bitcast(I32))
+        nc.sync.dma_start(out=tabw[1][:], in_=words_of(tab_words, 1))
+        load_w1(0)
+        nc.sync.dma_start(out=tabw[0][:], in_=words_of(tab_words, 0))
+        nc.sync.dma_start(out=bias[:], in_=b.rearrange("(g p t) -> p g t", g=2, t=4))
+        nc.sync.dma_start(p1[:], pos1)
+        nc.sync.dma_start(p2[:], pos2)
+        nc.sync.dma_start(out=gn[:], in_=gain.rearrange("(g p t) -> p g t", g=2, t=4))
+        nc.sync.dma_start(out=tr[:], in_=tried.rearrange("(g p t) -> p g t", g=2, t=4))
+        nc.sync.dma_start(idx2[:], offs2)
+        nc.sync.dma_start(out=tab2w[0][:], in_=words_of(tab2_words, 0))
+        load_w1(1)
+        for q in range(4):
+            nc.sync.dma_start(out=tab2s[32 * q : 32 * q + 8, :].bitcast(I32), in_=tab2_scales[:, 4 * q : 4 * q + 4, :].bitcast(I32))
+        nc.sync.dma_start(out=tab2w[1][:], in_=words_of(tab2_words, 1))
+        with nc.allow_non_contiguous_dma(reason="one value of veil for each partition"):
+            nc.sync.dma_start(out=vl[:], in_=veil.rearrange("(c p) -> p c", p=P))
+
+        for a in (1, 0):
+            for q in range(4):
+                r0 = 32 * q + 4 * (1 - a)
+                nc.gpsimd.dma_start(out=tabs[r0 : r0 + 4, :].bitcast(I32), in_=tab_scales[a, 4 * q : 4 * q + 4, :].bitcast(I32))
+
+        w4w = tile("w4w", [P, 2 * H], U8)
+        w4s = tile("w4s", [P, H], U8)
+        nc.vector.tensor_copy(
+            out=w4w[:].rearrange("p (g t m e) -> p g t m e", g=2, t=4, e=2),
+            in_=w4raw[:].rearrange("p (g m t e) -> p g t m e", g=2, t=4, e=2),
+        )
+        nc.vector.tensor_copy(
+            out=w4s[:].rearrange("p (g t m) -> p g t m", g=2, t=4),
+            in_=w4sraw[:].rearrange("p (g m t) -> p g t m", g=2, t=4),
+        )
+
+        vw = [tile("vw%d" % a, [P, S], U32) for a in range(2)]
+        vs = tile("vs", [P, S], U8)
+        nc.vector.tensor_copy(vw[1][:], tabw[1][:].bitcast(U32).indirect(idx[:]))
+        nc.vector.tensor_copy(vs[:], tabs[:].indirect(idx[:]))
+
+        w1w = [tile("w1w%d" % g, [P, 512], U32) for g in range(2)]
+        w1s = [tile("w1s%d" % g, [P, 512], U8) for g in range(2)]
+
+        def quantise_w1(g):
+            wb = tile("w1bf%d" % g, [P, 2048], BF16, tag="w1bf%d" % g)
+            nc.scalar.copy(
+                out=wb[:].rearrange("p (t m j) -> p m t j", t=4, j=4),
+                in_=w1raw[g][:].rearrange("p j (m t) -> p m t j", t=4),
+            )
+            nc.vector.quantize_mx(out=w1w[g][:].bitcast(FP8X4), scales=w1s[g][:], in_=wb[:])
+
+        quantise_w1(0)
+        for half in range(2):
+            nc.vector.tensor_copy(
+                vw[0][:, BANK * half : BANK * (half + 1)],
+                tabw[0][:].bitcast(U32).indirect(idx[:, 32 * half : 32 * (half + 1)]),
+            )
+
+        v2w = [tile("v2w%d" % a, [P, S2], U32) for a in range(2)]
+        v2s = tile("v2s", [P, S2], U8)
+        gt = tile("gt", [P, 2, 4], F32)
+        nc.vector.tensor_tensor(gt[:], gn[:], tr[:], ALU.mult)
+        nc.vector.tensor_copy(v2w[0][:], tab2w[0][:].bitcast(U32).indirect(idx2[:]))
+
+        hs = {}
+
+        def first_stage(g):
+            banks = {}
+            for t in range(4):
+                for half in range(2):
+                    acc = psum.tile([P, BANK], F32, name="acc", tag="bank")
+                    banks[t, half] = acc
+                    c0 = 512 * g + P * t
+                    cols = slice(BANK * half, BANK * (half + 1))
+                    nc.tensor.matmul_mx(
+                        out=acc[:],
+                        lhsT=w4w[:, 2 * c0 : 2 * c0 + 2 * P].bitcast(FP4X4),
+                        lhsT_scale=w4s[:, c0 : c0 + P],
+                        rhs=vw[1][:, cols].bitcast(FP8X4),
+                        rhs_scale=vs[:, cols],
+                        start=True,
+                        stop=False,
+                    )
+            for t in range(4):
+                h = tile("h%d%d" % (g, t), [P, S], F32)
+                hs[g, t] = h
+                for half in range(2):
+                    cols = slice(BANK * half, BANK * (half + 1))
+                    nc.tensor.matmul_mx(
+                        out=banks[t, half][:],
+                        lhsT=w1w[g][:, P * t : P * (t + 1)].bitcast(FP8X4),
+                        lhsT_scale=w1s[g][:, P * t : P * (t + 1)],
+                        rhs=vw[0][:, cols].bitcast(FP8X4),
+                        rhs_scale=vs[4:P, cols],
+                        start=False,
+                        stop=True,
+                    )
+                    nc.scalar.activation(out=h[:, cols], in_=banks[t, half][:], func=ACT.Silu, bias=bias[:, g, t : t + 1])
+
+        first_stage(0)
+        quantise_w1(1)
+        first_stage(1)
+
+        lists = (p1, p2)
+        factors = (gt, gn)
+
+        def pick(g, t, u, j0, j1, picked, rows):
+            nc.vector.tensor_copy(picked, hs[g, t][:].indirect(lists[u][:, j0 // 16 : j1 // 16]))
+            nc.scalar.activation(out=rows[:, t, :], in_=picked, func=ACT.Copy, scale=factors[u][:, g, t : t + 1])
+
+        def weave_and_quantise(name, rows, n, on_scalar):
+            xb = tile("xb" + name, [P, 4 * n], BF16)
+            dst = xb[:].rearrange("p (c i t) -> p c t i", i=4, t=4)
+            src = rows[:].rearrange("p t (c i) -> p c t i", i=4)
+            if on_scalar:
+                nc.scalar.copy(out=dst, in_=src)
+            else:
+                nc.vector.tensor_copy(out=dst, in_=src)
+            xw = tile("xw" + name, [P, n], U32)
+            xs = tile("xs" + name, [P, n], U8)
+            nc.vector.quantize_mx(out=xw[:].bitcast(FP8X4), scales=xs[:], in_=xb[:])
+            return xw, xs
+
+        rows0 = [tile("rows0%d" % u, [P, 4, NP], BF16) for u in range(2)]
+        for t in range(4):
+            both = tile("both%d" % t, [P, 2, NP], F32, tag="w1bf1" if t == 2 else None)
+            for u in range(2):
+                pick(0, t, u, 0, NP, both[:, u, :], rows0[u])
+        nc.vector.tensor_copy(v2s[:], tab2s[:].indirect(idx2[:]))
+        nc.vector.tensor_copy(v2w[1][:], tab2w[1][:].bitcast(U32).indirect(idx2[:]))
+
+        rows10 = tile("rows10", [P, 4, NP], BF16)
+        for t in range(4):
+            pk = tile("pk10%d" % t, [P, NP], F32)
+            pick(1, t, 0, 0, NP, pk[:], rows10)
+        x0 = [weave_and_quantise("0%d" % u, rows0[u], NP, True) for u in range(2)]
+
+        HALF = NP // 2
+        rows11 = [tile("rows11%d" % jh, [P, 4, HALF], BF16) for jh in range(2)]
+        for t in range(4):
+            pk = tile("pk110%d" % t, [P, HALF], F32)
+            pick(1, t, 1, 0, HALF, pk[:], rows11[0])
+        x10 = weave_and_quantise("10", rows10, NP, False)
+        for t in range(2):
+            pk = tile("pk111%d" % t, [P, HALF], F32)
+            pick(1, t, 1, HALF, NP, pk[:], rows11[1])
+        x11 = [weave_and_quantise("110", rows11[0], HALF, False)]
+        for t in range(2, 4):
+            pk = tile("pk111%d" % t, [P, HALF], F32)
+            pick(1, t, 1, HALF, NP, pk[:], rows11[1])
+        x11.append(weave_and_quantise("111", rows11[1], HALF, False))
+
+        out_v = out.rearrange("(c p) j -> p c j", p=P)
+        for jh in range(2):
+            cols = slice(HALF * jh, HALF * (jh + 1))
+            operands = [
+                (0, x0[0][0][:, cols], x0[0][1][:, cols]),
+                (0, x0[1][0][:, cols], x0[1][1][:, cols]),
+                (1, x10[0][:, cols], x10[1][:, cols]),
+                (1, x11[jh][0][:], x11[jh][1][:]),
+            ]
+            accs = [psum.tile([P, 2, HALF], F32, name="acc2", tag="bank") for mp in range(2)]
+            for n, (a, xw, xs) in enumerate(operands):
+                for c in range(4):
+                    nc.tensor.matmul_mx(
+                        out=accs[c // 2][:, c % 2, :],
+                        lhsT=v2w[a][:, P * c : P * (c + 1)].bitcast(FP8X4),
+                        lhsT_scale=v2s[4 * a : P, P * c : P * (c + 1)],
+                        rhs=xw.bitcast(FP8X4),
+                        rhs_scale=xs,
+                        start=(n == 0 and c % 2 == 0),
+                        stop=(n == 3 and c % 2 == 1),
+                    )
+            for mp in range(2):
+                res = tile("res%d%d" % (jh, mp), [P, 2, HALF], F32)
+                for e in range(2):
+                    c = 2 * mp + e
+                    if jh == 1 and mp == 1:
+                        nc.vector.tensor_scalar(out=res[:, e, :], in0=accs[mp][:, e, :], scalar1=vl[:, c : c + 1], scalar2=None, op0=ALU.mult)
+                    else:
+                        nc.scalar.activation(out=res[:, e, :], in_=accs[mp][:, e, :], func=ACT.Copy, scale=vl[:, c : c + 1])
+                nc.sync.dma_start(out=out_v[:, 2 * mp : 2 * mp + 2, cols], in_=res[:])

@@ -27,7 +27,8 @@ def tile_list_gown_veil_suggestion_kernel(
     nc = tc.nc
     with ExitStack() as ctx:
         keep = ctx.enter_context(tc.tile_pool(name="keep", bufs=1))
-        psum = ctx.enter_context(tc.psum_pool(name="psum", bufs=8))
+        turns = ctx.enter_context(tc.tile_pool(name="turns", bufs=1))
+        psum = ctx.enter_context(tc.psum_pool(name="psum", bufs=4))
 
         def tile(name, shape, dtype, tag=None):
             return keep.tile(shape, dtype, name=name, tag=tag or name, align_bytes=64)
@@ -39,103 +40,112 @@ def tile_list_gown_veil_suggestion_kernel(
         idx2 = tile("idx2", [P, S2 // 16], U16)
         p1 = tile("p1", [P, NP // 16], U16)
         p2 = tile("p2", [P, NP // 16], U16)
-        tabw = [tile("tabw%d" % a, [P, T], I32) for a in range(2)]
+        tabw1 = tile("tabw1", [P, T], I32)
         tabs = tile("tabs", [P, T], U8)
-        tab2w = [tile("tab2w%d" % a, [P, T3], I32) for a in range(2)]
-        tab2s = tile("tab2s", [P, T3], U8)
         w4raw = tile("w4raw", [P, 2 * H], U8)
-        w4sraw = tile("w4sraw", [P, H], U8)
-        w1raw = [tile("w1raw%d" % g, [P, 4, 512], F32) for g in range(2)]
-        bias = tile("bias", [P, 2, 4], F32)
-        gn = tile("gn", [P, 2, 4], F32)
-        tr = tile("tr", [P, 2, 4], F32)
-        vl = tile("vl", [P, 4], F32)
+        w4sraw = turns.tile([P, H], U8, name="w4sraw", align_bytes=64, offset=4 * T + T3 - 512)
+        w1raw0 = turns.tile([P, 4, 512], F32, name="w1raw0", align_bytes=64, offset=0)
 
         nc.vector.memset(w4sraw[:].bitcast(I32), 0)
         nc.vector.memset(tabs[:].bitcast(I32), 0)
-        nc.vector.memset(tab2s[:].bitcast(I32), 0)
 
-        def load_w1(g):
-            nc.sync.dma_start(out=w1raw[g][:], in_=w1[:, 512 * g : 512 * g + 512].rearrange("(p j) c -> p j c", j=4))
+        def load_w1(g, raw):
+            nc.sync.dma_start(out=raw[:], in_=w1[:, 512 * g : 512 * g + 512].rearrange("(p j) c -> p j c", j=4))
 
-        nc.sync.dma_start(idx[:], offs)
+        def load_tab_scales(queue, a, q):
+            r0 = 32 * q + 4 * (1 - a)
+            queue.dma_start(out=tabs[r0 : r0 + 4, :].bitcast(I32), in_=tab_scales[a, 4 * q : 4 * q + 4, :].bitcast(I32))
+
         nc.sync.dma_start(out=w4raw[:].bitcast(I32), in_=w4_words[0].bitcast(I32))
-        for q in range(4):
-            nc.sync.dma_start(out=w4sraw[32 * q : 32 * q + 4, :].bitcast(I32), in_=w4_scales[0, 4 * q : 4 * q + 4, :].bitcast(I32))
-        nc.sync.dma_start(out=tabw[1][:], in_=words_of(tab_words, 1))
-        load_w1(0)
-        nc.sync.dma_start(out=tabw[0][:], in_=words_of(tab_words, 0))
-        nc.sync.dma_start(out=bias[:], in_=b.rearrange("(g p t) -> p g t", g=2, t=4))
+        nc.sync.dma_start(idx[:], offs)
         nc.sync.dma_start(p1[:], pos1)
         nc.sync.dma_start(p2[:], pos2)
-        nc.sync.dma_start(out=gn[:], in_=gain.rearrange("(g p t) -> p g t", g=2, t=4))
-        nc.sync.dma_start(out=tr[:], in_=tried.rearrange("(g p t) -> p g t", g=2, t=4))
         nc.sync.dma_start(idx2[:], offs2)
-        nc.sync.dma_start(out=tab2w[0][:], in_=words_of(tab2_words, 0))
-        load_w1(1)
+        load_w1(0, w1raw0)
         for q in range(4):
-            nc.sync.dma_start(out=tab2s[32 * q : 32 * q + 8, :].bitcast(I32), in_=tab2_scales[:, 4 * q : 4 * q + 4, :].bitcast(I32))
-        nc.sync.dma_start(out=tab2w[1][:], in_=words_of(tab2_words, 1))
-        with nc.allow_non_contiguous_dma(reason="one value of veil for each partition"):
-            nc.sync.dma_start(out=vl[:], in_=veil.rearrange("(c p) -> p c", p=P))
-
-        for a in (1, 0):
-            for q in range(4):
-                r0 = 32 * q + 4 * (1 - a)
-                nc.gpsimd.dma_start(out=tabs[r0 : r0 + 4, :].bitcast(I32), in_=tab_scales[a, 4 * q : 4 * q + 4, :].bitcast(I32))
+            nc.sync.dma_start(out=w4sraw[32 * q : 32 * q + 4, :].bitcast(I32), in_=w4_scales[0, 4 * q : 4 * q + 4, :].bitcast(I32))
+        nc.sync.dma_start(out=tabw1[:], in_=words_of(tab_words, 1))
+        for n in range(8):
+            load_tab_scales(nc.gpsimd if n < 2 else nc.sync, n % 2, n // 2)
 
         w4w = tile("w4w", [P, 2 * H], U8)
-        w4s = tile("w4s", [P, H], U8)
         nc.vector.tensor_copy(
-            out=w4w[:].rearrange("p (g t m e) -> p g t m e", g=2, t=4, e=2),
-            in_=w4raw[:].rearrange("p (g m t e) -> p g t m e", g=2, t=4, e=2),
-        )
-        nc.vector.tensor_copy(
-            out=w4s[:].rearrange("p (g t m) -> p g t m", g=2, t=4),
-            in_=w4sraw[:].rearrange("p (g m t) -> p g t m", g=2, t=4),
+            out=w4w[:].bitcast(U16).rearrange("p (g t m) -> p g t m", g=2, t=4),
+            in_=w4raw[:].bitcast(U16).rearrange("p (g m t) -> p g t m", g=2, t=4),
         )
 
-        vw = [tile("vw%d" % a, [P, S], U32) for a in range(2)]
-        vs = tile("vs", [P, S], U8)
-        nc.vector.tensor_copy(vw[1][:], tabw[1][:].bitcast(U32).indirect(idx[:]))
-        nc.vector.tensor_copy(vs[:], tabs[:].indirect(idx[:]))
+        consts = tile("consts", [P, 4, 8], F32, tag="w4raw")
+        bias, gn, tr, vl = (consts[:, n, :] for n in range(4))
+        for vec, dst in ((b, bias), (gain, gn), (tried, tr)):
+            nc.gpsimd.dma_start(out=dst.rearrange("p (g t) -> p g t", g=2), in_=vec.rearrange("(g p t) -> p g t", g=2, t=4))
+        with nc.allow_non_contiguous_dma(reason="one value of veil for each partition"):
+            nc.gpsimd.dma_start(out=vl[:, 0:4], in_=veil.rearrange("(c p) -> p c", p=P))
+        gt = tile("gt", [P, 8], F32)
+        nc.gpsimd.tensor_tensor(gt[:], gn, tr, ALU.mult)
 
         w1w = [tile("w1w%d" % g, [P, 512], U32) for g in range(2)]
         w1s = [tile("w1s%d" % g, [P, 512], U8) for g in range(2)]
 
-        def quantise_w1(g):
-            wb = tile("w1bf%d" % g, [P, 2048], BF16, tag="w1bf%d" % g)
-            nc.scalar.copy(
-                out=wb[:].rearrange("p (t m j) -> p m t j", t=4, j=4),
-                in_=w1raw[g][:].rearrange("p j (m t) -> p m t j", t=4),
-            )
+        def weave_w1(g, raw):
+            wb = tile("w1bf%d" % g, [P, 2048], BF16)
+            dst = wb[:].rearrange("p (t m j) -> p m t j", t=4, j=4)
+            src = raw[:].rearrange("p j (m t) -> p m t j", t=4)
+            if g == 0:
+                nc.vector.tensor_copy(out=dst, in_=src)
+            else:
+                nc.scalar.copy(out=dst, in_=src)
+            return wb
+
+        def quantise_w1(g, wb):
             nc.vector.quantize_mx(out=w1w[g][:].bitcast(FP8X4), scales=w1s[g][:], in_=wb[:])
 
-        quantise_w1(0)
+        wb0 = weave_w1(0, w1raw0)
+        tabw0 = turns.tile([P, T], I32, name="tabw0", align_bytes=64, offset=0)
+        nc.sync.dma_start(out=tabw0[:], in_=words_of(tab_words, 0))
+        quantise_w1(0, wb0)
+        w4s = tile("w4s", [P, H], U8, tag="w1bf0")
+        nc.vector.tensor_copy(
+            out=w4s[:].rearrange("p (g t m) -> p g t m", g=2, t=4),
+            in_=w4sraw[:].rearrange("p (g m t) -> p g t m", g=2, t=4),
+        )
+        tab2s = turns.tile([P, T3], U8, name="tab2s", align_bytes=64, offset=4 * T)
+        nc.vector.memset(tab2s[:].bitcast(I32), 0)
+        for q in range(4):
+            nc.sync.dma_start(out=tab2s[32 * q : 32 * q + 8, :].bitcast(I32), in_=tab2_scales[:, 4 * q : 4 * q + 4, :].bitcast(I32))
+        tab2w0 = turns.tile([P, T3], I32, name="tab2w0", align_bytes=64, offset=4 * T + T3)
+        nc.sync.dma_start(out=tab2w0[:], in_=words_of(tab2_words, 0))
+
+        vw = [tile("vw%d" % a, [P, S], U32) for a in range(2)]
+        vs = tile("vs", [P, S], U8)
+        nc.vector.tensor_copy(vw[1][:], tabw1[:].bitcast(U32).indirect(idx[:]))
+        nc.vector.tensor_copy(vs[:], tabs[:].indirect(idx[:]))
+        w1raw1 = tile("w1raw1", [P, 4, 512], F32, tag="tabs")
+        load_w1(1, w1raw1)
         for half in range(2):
             nc.vector.tensor_copy(
                 vw[0][:, BANK * half : BANK * (half + 1)],
-                tabw[0][:].bitcast(U32).indirect(idx[:, 32 * half : 32 * (half + 1)]),
+                tabw0[:].bitcast(U32).indirect(idx[:, 32 * half : 32 * (half + 1)]),
             )
+        tab2w1 = turns.tile([P, T3], I32, name="tab2w1", align_bytes=64, offset=0)
+        nc.sync.dma_start(out=tab2w1[:], in_=words_of(tab2_words, 1))
 
         v2w = [tile("v2w%d" % a, [P, S2], U32) for a in range(2)]
-        v2s = tile("v2s", [P, S2], U8)
-        gt = tile("gt", [P, 2, 4], F32)
-        nc.vector.tensor_tensor(gt[:], gn[:], tr[:], ALU.mult)
-        nc.vector.tensor_copy(v2w[0][:], tab2w[0][:].bitcast(U32).indirect(idx2[:]))
+        v2s = turns.tile([P, S2], U8, name="v2s", align_bytes=64, offset=4 * T3)
+        nc.vector.tensor_copy(v2s[:], tab2s[:].indirect(idx2[:]))
+        nc.vector.tensor_copy(v2w[0][:], tab2w0[:].bitcast(U32).indirect(idx2[:]))
 
         hs = {}
 
         def first_stage(g):
-            banks = {}
             for t in range(4):
+                h = tile("h%d%d" % (g, t), [P, S], F32)
+                hs[g, t] = h
+                c0 = 512 * g + P * t
+                banks = [psum.tile([P, BANK], F32, name="acc", tag="first") for half in range(2)]
                 for half in range(2):
-                    acc = psum.tile([P, BANK], F32, name="acc", tag="bank")
-                    banks[t, half] = acc
-                    c0 = 512 * g + P * t
                     cols = slice(BANK * half, BANK * (half + 1))
                     nc.tensor.matmul_mx(
-                        out=acc[:],
+                        out=banks[half][:],
                         lhsT=w4w[:, 2 * c0 : 2 * c0 + 2 * P].bitcast(FP4X4),
                         lhsT_scale=w4s[:, c0 : c0 + P],
                         rhs=vw[1][:, cols].bitcast(FP8X4),
@@ -143,13 +153,10 @@ def tile_list_gown_veil_suggestion_kernel(
                         start=True,
                         stop=False,
                     )
-            for t in range(4):
-                h = tile("h%d%d" % (g, t), [P, S], F32)
-                hs[g, t] = h
                 for half in range(2):
                     cols = slice(BANK * half, BANK * (half + 1))
                     nc.tensor.matmul_mx(
-                        out=banks[t, half][:],
+                        out=banks[half][:],
                         lhsT=w1w[g][:, P * t : P * (t + 1)].bitcast(FP8X4),
                         lhsT_scale=w1s[g][:, P * t : P * (t + 1)],
                         rhs=vw[0][:, cols].bitcast(FP8X4),
@@ -157,20 +164,22 @@ def tile_list_gown_veil_suggestion_kernel(
                         start=False,
                         stop=True,
                     )
-                    nc.scalar.activation(out=h[:, cols], in_=banks[t, half][:], func=ACT.Silu, bias=bias[:, g, t : t + 1])
+                    nc.scalar.activation(out=h[:, cols], in_=banks[half][:], func=ACT.Silu, bias=bias[:, 4 * g + t : 4 * g + t + 1])
 
         first_stage(0)
-        quantise_w1(1)
+        quantise_w1(1, weave_w1(1, w1raw1))
         first_stage(1)
 
         lists = (p1, p2)
         factors = (gt, gn)
 
-        def pick(g, t, u, j0, j1, picked, rows):
+        def pick(g, t, u, j0, j1, picked):
             nc.vector.tensor_copy(picked, hs[g, t][:].indirect(lists[u][:, j0 // 16 : j1 // 16]))
-            nc.scalar.activation(out=rows[:, t, :], in_=picked, func=ACT.Copy, scale=factors[u][:, g, t : t + 1])
 
-        def weave_and_quantise(name, rows, n, on_scalar):
+        def scale(g, t, u, picked, rows):
+            nc.scalar.activation(out=rows[:, t, :], in_=picked, func=ACT.Copy, scale=factors[u][:, 4 * g + t : 4 * g + t + 1])
+
+        def weave(name, rows, n, on_scalar):
             xb = tile("xb" + name, [P, 4 * n], BF16)
             dst = xb[:].rearrange("p (c i t) -> p c t i", i=4, t=4)
             src = rows[:].rearrange("p t (c i) -> p c t i", i=4)
@@ -178,67 +187,80 @@ def tile_list_gown_veil_suggestion_kernel(
                 nc.scalar.copy(out=dst, in_=src)
             else:
                 nc.vector.tensor_copy(out=dst, in_=src)
+            return xb
+
+        def quantise(name, xb, n):
             xw = tile("xw" + name, [P, n], U32)
             xs = tile("xs" + name, [P, n], U8)
             nc.vector.quantize_mx(out=xw[:].bitcast(FP8X4), scales=xs[:], in_=xb[:])
             return xw, xs
 
+        HALF = NP // 2
         rows0 = [tile("rows0%d" % u, [P, 4, NP], BF16) for u in range(2)]
         for t in range(4):
             both = tile("both%d" % t, [P, 2, NP], F32, tag="w1bf1" if t == 2 else None)
             for u in range(2):
-                pick(0, t, u, 0, NP, both[:, u, :], rows0[u])
-        nc.vector.tensor_copy(v2s[:], tab2s[:].indirect(idx2[:]))
-        nc.vector.tensor_copy(v2w[1][:], tab2w[1][:].bitcast(U32).indirect(idx2[:]))
+                pick(0, t, u, 0, NP, both[:, u, :])
+                scale(0, t, u, both[:, u, :], rows0[u])
+            if t == 1:
+                nc.vector.tensor_copy(v2w[1][:], tab2w1[:].bitcast(U32).indirect(idx2[:]))
+
+        pk10 = [tile("pk10%d" % t, [P, NP], F32) for t in range(4)]
+        pk110 = [tile("pk110%d" % t, [P, HALF], F32) for t in range(4)]
+        for t in range(4):
+            pick(1, t, 0, 0, NP, pk10[t][:])
+        for t in range(4):
+            pick(1, t, 1, 0, HALF, pk110[t][:])
+        x00 = quantise("00", weave("00", rows0[0], NP, True), NP)
+        pk111 = tile("pk111", [P, 4, HALF], F32, tag="xb00")
+        for t in range(4):
+            pick(1, t, 1, HALF, NP, pk111[:, t, :])
+        x01 = quantise("01", weave("01", rows0[1], NP, True), NP)
 
         rows10 = tile("rows10", [P, 4, NP], BF16)
-        for t in range(4):
-            pk = tile("pk10%d" % t, [P, NP], F32)
-            pick(1, t, 0, 0, NP, pk[:], rows10)
-        x0 = [weave_and_quantise("0%d" % u, rows0[u], NP, True) for u in range(2)]
-
-        HALF = NP // 2
         rows11 = [tile("rows11%d" % jh, [P, 4, HALF], BF16) for jh in range(2)]
         for t in range(4):
-            pk = tile("pk110%d" % t, [P, HALF], F32)
-            pick(1, t, 1, 0, HALF, pk[:], rows11[0])
-        x10 = weave_and_quantise("10", rows10, NP, False)
-        for t in range(2):
-            pk = tile("pk111%d" % t, [P, HALF], F32)
-            pick(1, t, 1, HALF, NP, pk[:], rows11[1])
-        x11 = [weave_and_quantise("110", rows11[0], HALF, False)]
-        for t in range(2, 4):
-            pk = tile("pk111%d" % t, [P, HALF], F32)
-            pick(1, t, 1, HALF, NP, pk[:], rows11[1])
-        x11.append(weave_and_quantise("111", rows11[1], HALF, False))
+            scale(1, t, 0, pk10[t][:], rows10)
+        xb10 = weave("10", rows10, NP, False)
+        for t in range(4):
+            scale(1, t, 1, pk110[t][:], rows11[0])
+        for t in range(4):
+            scale(1, t, 1, pk111[:, t, :], rows11[1])
+        x10 = quantise("10", xb10, NP)
+        xb110 = weave("110", rows11[0], HALF, False)
+        xb111 = weave("111", rows11[1], HALF, True)
+        x110 = quantise("110", xb110, HALF)
+        x111 = quantise("111", xb111, HALF)
+        x11 = [x110, x111]
 
         out_v = out.rearrange("(c p) j -> p c j", p=P)
+        accs = {}
         for jh in range(2):
-            cols = slice(HALF * jh, HALF * (jh + 1))
-            operands = [
-                (0, x0[0][0][:, cols], x0[0][1][:, cols]),
-                (0, x0[1][0][:, cols], x0[1][1][:, cols]),
-                (1, x10[0][:, cols], x10[1][:, cols]),
-                (1, x11[jh][0][:], x11[jh][1][:]),
-            ]
-            accs = [psum.tile([P, 2, HALF], F32, name="acc2", tag="bank") for mp in range(2)]
-            for n, (a, xw, xs) in enumerate(operands):
+            for mp in range(2):
+                accs[jh, mp] = psum.tile([P, 2, HALF], F32, name="acc2", tag="second")
+        for n, a in enumerate((0, 0, 1, 1)):
+            for jh in range(2):
+                cols = slice(HALF * jh, HALF * (jh + 1))
+                xw, xs = (x00, x01, x10, x11[jh])[n]
+                xcols = cols if n < 3 else slice(0, HALF)
                 for c in range(4):
                     nc.tensor.matmul_mx(
-                        out=accs[c // 2][:, c % 2, :],
+                        out=accs[jh, c // 2][:, c % 2, :],
                         lhsT=v2w[a][:, P * c : P * (c + 1)].bitcast(FP8X4),
                         lhsT_scale=v2s[4 * a : P, P * c : P * (c + 1)],
-                        rhs=xw.bitcast(FP8X4),
-                        rhs_scale=xs,
+                        rhs=xw[:, xcols].bitcast(FP8X4),
+                        rhs_scale=xs[:, xcols],
                         start=(n == 0 and c % 2 == 0),
                         stop=(n == 3 and c % 2 == 1),
                     )
+        for jh in range(2):
+            cols = slice(HALF * jh, HALF * (jh + 1))
             for mp in range(2):
                 res = tile("res%d%d" % (jh, mp), [P, 2, HALF], F32)
                 for e in range(2):
                     c = 2 * mp + e
-                    if jh == 1 and mp == 1:
-                        nc.vector.tensor_scalar(out=res[:, e, :], in0=accs[mp][:, e, :], scalar1=vl[:, c : c + 1], scalar2=None, op0=ALU.mult)
+                    if mp == 1:
+                        nc.vector.tensor_scalar(out=res[:, e, :], in0=accs[jh, mp][:, e, :], scalar1=vl[:, c : c + 1], scalar2=None, op0=ALU.mult)
                     else:
-                        nc.scalar.activation(out=res[:, e, :], in_=accs[mp][:, e, :], func=ACT.Copy, scale=vl[:, c : c + 1])
+                        nc.scalar.activation(out=res[:, e, :], in_=accs[jh, mp][:, e, :], func=ACT.Copy, scale=vl[:, c : c + 1])
                 nc.sync.dma_start(out=out_v[:, 2 * mp : 2 * mp + 2, cols], in_=res[:])

@@ -2,7 +2,7 @@ from contextlib import ExitStack
 
 import concourse.mybir as mybir
 
-K, K1, H, T, S, S2, T3, NP = 1024, 512, 1024, 4096, 1024, 512, 2048, 512
+K, H, T, S, S2, T3, NP = 1024, 1024, 4096, 1024, 512, 2048, 512
 FLOPS = 2 * K * H * S + 2 * 2 * H * S2 * NP
 
 F32 = mybir.dt.float32
@@ -17,7 +17,21 @@ ACT = mybir.ActivationFunctionType
 ALU = mybir.AluOpType
 
 P = 128
+PACK = 4
+PASS = P * PACK
 BANK = 512
+QUAD = 32
+GROUP = 16
+HALF = NP // 2
+TAB_SCALE_LOADS_ON_GPSIMD = 2
+SLICES_BEFORE_W1_QUANTISE = 2
+
+AT_TAB_PASS0 = 0
+AT_V2_SCALES = 4 * T3
+AT_TAB2_SCALES = 4 * T
+AT_W4_SCALES_RAW = AT_TAB2_SCALES + T3 - H // 2
+AT_TAB2_PASS0 = AT_TAB2_SCALES + T3
+AT_TAB_SCALES = AT_TAB2_PASS0 + 4 * T3
 
 
 def tile_list_gown_veil_suggestion_kernel(
@@ -33,28 +47,30 @@ def tile_list_gown_veil_suggestion_kernel(
         def tile(name, shape, dtype, tag=None):
             return keep.tile(shape, dtype, name=name, tag=tag or name, align_bytes=64)
 
+        def placed(name, shape, dtype, offset):
+            return turns.tile(shape, dtype, name=name, align_bytes=64, offset=offset)
+
         def words_of(table, a):
             return table[a].rearrange("p t i -> p (t i)").bitcast(I32)
 
-        idx = tile("idx", [P, S // 16], U16)
-        idx2 = tile("idx2", [P, S2 // 16], U16)
-        p1 = tile("p1", [P, NP // 16], U16)
-        p2 = tile("p2", [P, NP // 16], U16)
+        idx = tile("idx", [P, S // GROUP], U16)
+        idx2 = tile("idx2", [P, S2 // GROUP], U16)
+        p1 = tile("p1", [P, NP // GROUP], U16)
+        p2 = tile("p2", [P, NP // GROUP], U16)
         tabw1 = tile("tabw1", [P, T], I32)
-        tabs = tile("tabs", [P, T], U8)
+        tabs = placed("tabs", [P, T], U8, AT_TAB_SCALES)
         w4raw = tile("w4raw", [P, 2 * H], U8)
-        w4sraw = turns.tile([P, H], U8, name="w4sraw", align_bytes=64, offset=4 * T + T3 - 512)
-        w1raw0 = turns.tile([P, 4, 512], F32, name="w1raw0", align_bytes=64, offset=0)
+        w4sraw = placed("w4sraw", [P, H], U8, AT_W4_SCALES_RAW)
+        w1raw0 = placed("w1raw0", [P, PACK, PASS], F32, AT_TAB_PASS0)
 
         nc.vector.memset(w4sraw[:].bitcast(I32), 0)
         nc.vector.memset(tabs[:].bitcast(I32), 0)
 
         def load_w1(g, raw):
-            nc.sync.dma_start(out=raw[:], in_=w1[:, 512 * g : 512 * g + 512].rearrange("(p j) c -> p j c", j=4))
+            nc.sync.dma_start(out=raw[:], in_=w1[:, PASS * g : PASS * (g + 1)].rearrange("(p i) c -> p i c", i=PACK))
 
-        def load_tab_scales(queue, a, q):
-            r0 = 32 * q + 4 * (1 - a)
-            queue.dma_start(out=tabs[r0 : r0 + 4, :].bitcast(I32), in_=tab_scales[a, 4 * q : 4 * q + 4, :].bitcast(I32))
+        def load_scale_rows(queue, plane, first, scales, r):
+            queue.dma_start(out=plane[first + r : P : QUAD, :].bitcast(I32), in_=scales[r : PACK * PACK : PACK, :].bitcast(I32))
 
         nc.sync.dma_start(out=w4raw[:].bitcast(I32), in_=w4_words[0].bitcast(I32))
         nc.sync.dma_start(idx[:], offs)
@@ -62,91 +78,95 @@ def tile_list_gown_veil_suggestion_kernel(
         nc.sync.dma_start(p2[:], pos2)
         nc.sync.dma_start(idx2[:], offs2)
         load_w1(0, w1raw0)
-        for q in range(4):
-            nc.sync.dma_start(out=w4sraw[32 * q : 32 * q + 4, :].bitcast(I32), in_=w4_scales[0, 4 * q : 4 * q + 4, :].bitcast(I32))
+        for r in range(PACK):
+            load_scale_rows(nc.sync, w4sraw, 0, w4_scales[0], r)
         nc.sync.dma_start(out=tabw1[:], in_=words_of(tab_words, 1))
-        for n in range(8):
-            load_tab_scales(nc.gpsimd if n < 2 else nc.sync, n % 2, n // 2)
+        for n in range(2 * PACK):
+            a, r = n % 2, n // 2
+            queue = nc.gpsimd if n < TAB_SCALE_LOADS_ON_GPSIMD else nc.sync
+            load_scale_rows(queue, tabs, PACK * (1 - a), tab_scales[a], r)
 
         w4w = tile("w4w", [P, 2 * H], U8)
         nc.vector.tensor_copy(
-            out=w4w[:].bitcast(U16).rearrange("p (g t m) -> p g t m", g=2, t=4),
-            in_=w4raw[:].bitcast(U16).rearrange("p (g m t) -> p g t m", g=2, t=4),
+            out=w4w[:].bitcast(U16).rearrange("p (g t m) -> p g t m", g=2, t=PACK),
+            in_=w4raw[:].bitcast(U16).rearrange("p (g m t) -> p g t m", g=2, t=PACK),
         )
 
         consts = tile("consts", [P, 4, 8], F32, tag="w4raw")
-        bias, gn, tr, vl = (consts[:, n, :] for n in range(4))
-        for vec, dst in ((b, bias), (gain, gn), (tried, tr)):
-            nc.gpsimd.dma_start(out=dst.rearrange("p (g t) -> p g t", g=2), in_=vec.rearrange("(g p t) -> p g t", g=2, t=4))
+        bias, gain_sb, tried_sb, veil_sb = (consts[:, n, :] for n in range(4))
+        for vec, dst in ((b, bias), (gain, gain_sb), (tried, tried_sb)):
+            nc.gpsimd.dma_start(out=dst.rearrange("p (g t) -> p g t", g=2), in_=vec.rearrange("(g p t) -> p g t", g=2, t=PACK))
         with nc.allow_non_contiguous_dma(reason="one value of veil for each partition"):
-            nc.gpsimd.dma_start(out=vl[:, 0:4], in_=veil.rearrange("(c p) -> p c", p=P))
-        gt = tile("gt", [P, 8], F32)
-        nc.gpsimd.tensor_tensor(gt[:], gn, tr, ALU.mult)
+            nc.gpsimd.dma_start(out=veil_sb[:, 0 : S2 // P], in_=veil.rearrange("(c p) -> p c", p=P))
+        gain_tried = tile("gt", [P, 8], F32)
+        nc.gpsimd.tensor_tensor(gain_tried[:], gain_sb, tried_sb, ALU.mult)
 
-        w1w = [tile("w1w%d" % g, [P, 512], U32) for g in range(2)]
-        w1s = [tile("w1s%d" % g, [P, 512], U8) for g in range(2)]
+        w1w = [tile("w1w%d" % g, [P, PASS], U32) for g in range(2)]
+        w1s = [tile("w1s%d" % g, [P, PASS], U8) for g in range(2)]
 
-        def weave_w1(g, raw):
-            wb = tile("w1bf%d" % g, [P, 2048], BF16)
-            dst = wb[:].rearrange("p (t m j) -> p m t j", t=4, j=4)
-            src = raw[:].rearrange("p j (m t) -> p m t j", t=4)
-            if g == 0:
-                nc.vector.tensor_copy(out=dst, in_=src)
-            else:
-                nc.scalar.copy(out=dst, in_=src)
+        def weave_w1(g, raw, copy):
+            wb = tile("w1bf%d" % g, [P, PACK * PASS], BF16)
+            copy(
+                out=wb[:].rearrange("p (t m i) -> p m t i", t=PACK, i=PACK),
+                in_=raw[:].rearrange("p i (m t) -> p m t i", t=PACK),
+            )
             return wb
 
         def quantise_w1(g, wb):
             nc.vector.quantize_mx(out=w1w[g][:].bitcast(FP8X4), scales=w1s[g][:], in_=wb[:])
 
-        wb0 = weave_w1(0, w1raw0)
-        tabw0 = turns.tile([P, T], I32, name="tabw0", align_bytes=64, offset=0)
+        wb0 = weave_w1(0, w1raw0, nc.vector.tensor_copy)
+        tabw0 = placed("tabw0", [P, T], I32, AT_TAB_PASS0)
         nc.sync.dma_start(out=tabw0[:], in_=words_of(tab_words, 0))
         quantise_w1(0, wb0)
         w4s = tile("w4s", [P, H], U8, tag="w1bf0")
         nc.vector.tensor_copy(
-            out=w4s[:].rearrange("p (g t m) -> p g t m", g=2, t=4),
-            in_=w4sraw[:].rearrange("p (g m t) -> p g t m", g=2, t=4),
+            out=w4s[:].rearrange("p (g t m) -> p g t m", g=2, t=PACK),
+            in_=w4sraw[:].rearrange("p (g m t) -> p g t m", g=2, t=PACK),
         )
-        tab2s = turns.tile([P, T3], U8, name="tab2s", align_bytes=64, offset=4 * T)
+
+        tab2s = placed("tab2s", [P, T3], U8, AT_TAB2_SCALES)
         nc.vector.memset(tab2s[:].bitcast(I32), 0)
-        for q in range(4):
-            nc.sync.dma_start(out=tab2s[32 * q : 32 * q + 8, :].bitcast(I32), in_=tab2_scales[:, 4 * q : 4 * q + 4, :].bitcast(I32))
-        tab2w0 = turns.tile([P, T3], I32, name="tab2w0", align_bytes=64, offset=4 * T + T3)
+        for q in range(P // QUAD):
+            nc.sync.dma_start(
+                out=tab2s[QUAD * q : QUAD * q + 2 * PACK, :].bitcast(I32),
+                in_=tab2_scales[:, PACK * q : PACK * (q + 1), :].bitcast(I32),
+            )
+        tab2w0 = placed("tab2w0", [P, T3], I32, AT_TAB2_PASS0)
         nc.sync.dma_start(out=tab2w0[:], in_=words_of(tab2_words, 0))
 
         vw = [tile("vw%d" % a, [P, S], U32) for a in range(2)]
         vs = tile("vs", [P, S], U8)
         nc.vector.tensor_copy(vw[1][:], tabw1[:].bitcast(U32).indirect(idx[:]))
         nc.vector.tensor_copy(vs[:], tabs[:].indirect(idx[:]))
-        w1raw1 = tile("w1raw1", [P, 4, 512], F32, tag="tabs")
+        w1raw1 = placed("w1raw1", [P, PACK, PASS], F32, AT_TAB_SCALES)
         load_w1(1, w1raw1)
         for half in range(2):
             nc.vector.tensor_copy(
                 vw[0][:, BANK * half : BANK * (half + 1)],
-                tabw0[:].bitcast(U32).indirect(idx[:, 32 * half : 32 * (half + 1)]),
+                tabw0[:].bitcast(U32).indirect(idx[:, BANK // GROUP * half : BANK // GROUP * (half + 1)]),
             )
-        tab2w1 = turns.tile([P, T3], I32, name="tab2w1", align_bytes=64, offset=0)
+        tab2w1 = placed("tab2w1", [P, T3], I32, AT_TAB_PASS0)
         nc.sync.dma_start(out=tab2w1[:], in_=words_of(tab2_words, 1))
 
         v2w = [tile("v2w%d" % a, [P, S2], U32) for a in range(2)]
-        v2s = turns.tile([P, S2], U8, name="v2s", align_bytes=64, offset=4 * T3)
+        v2s = placed("v2s", [P, S2], U8, AT_V2_SCALES)
         nc.vector.tensor_copy(v2s[:], tab2s[:].indirect(idx2[:]))
         nc.vector.tensor_copy(v2w[0][:], tab2w0[:].bitcast(U32).indirect(idx2[:]))
 
-        hs = {}
+        slices = {}
 
-        def first_stage(g):
-            for t in range(4):
-                h = tile("h%d%d" % (g, t), [P, S], F32)
-                hs[g, t] = h
-                c0 = 512 * g + P * t
+        def first_product(g):
+            for t in range(PACK):
+                act = tile("h%d%d" % (g, t), [P, S], F32)
+                slices[g, t] = act
+                c0 = PASS * g + P * t
                 banks = [psum.tile([P, BANK], F32, name="acc", tag="first") for half in range(2)]
                 for half in range(2):
                     cols = slice(BANK * half, BANK * (half + 1))
                     nc.tensor.matmul_mx(
                         out=banks[half][:],
-                        lhsT=w4w[:, 2 * c0 : 2 * c0 + 2 * P].bitcast(FP4X4),
+                        lhsT=w4w[:, 2 * c0 : 2 * (c0 + P)].bitcast(FP4X4),
                         lhsT_scale=w4s[:, c0 : c0 + P],
                         rhs=vw[1][:, cols].bitcast(FP8X4),
                         rhs_scale=vs[:, cols],
@@ -160,107 +180,104 @@ def tile_list_gown_veil_suggestion_kernel(
                         lhsT=w1w[g][:, P * t : P * (t + 1)].bitcast(FP8X4),
                         lhsT_scale=w1s[g][:, P * t : P * (t + 1)],
                         rhs=vw[0][:, cols].bitcast(FP8X4),
-                        rhs_scale=vs[4:P, cols],
+                        rhs_scale=vs[PACK:P, cols],
                         start=False,
                         stop=True,
                     )
-                    nc.scalar.activation(out=h[:, cols], in_=banks[half][:], func=ACT.Silu, bias=bias[:, 4 * g + t : 4 * g + t + 1])
+                    n = PACK * g + t
+                    nc.scalar.activation(out=act[:, cols], in_=banks[half][:], func=ACT.Silu, bias=bias[:, n : n + 1])
 
-        first_stage(0)
-        quantise_w1(1, weave_w1(1, w1raw1))
-        first_stage(1)
+        first_product(0)
+        quantise_w1(1, weave_w1(1, w1raw1, nc.scalar.copy))
+        first_product(1)
 
         lists = (p1, p2)
-        factors = (gt, gn)
+        factors = (gain_tried, gain_sb)
 
         def pick(g, t, u, j0, j1, picked):
-            nc.vector.tensor_copy(picked, hs[g, t][:].indirect(lists[u][:, j0 // 16 : j1 // 16]))
+            nc.vector.tensor_copy(picked, slices[g, t][:].indirect(lists[u][:, j0 // GROUP : j1 // GROUP]))
 
         def scale(g, t, u, picked, rows):
-            nc.scalar.activation(out=rows[:, t, :], in_=picked, func=ACT.Copy, scale=factors[u][:, 4 * g + t : 4 * g + t + 1])
+            n = PACK * g + t
+            nc.scalar.activation(out=rows[:, t, :], in_=picked, func=ACT.Copy, scale=factors[u][:, n : n + 1])
 
-        def weave(name, rows, n, on_scalar):
-            xb = tile("xb" + name, [P, 4 * n], BF16)
-            dst = xb[:].rearrange("p (c i t) -> p c t i", i=4, t=4)
-            src = rows[:].rearrange("p t (c i) -> p c t i", i=4)
-            if on_scalar:
-                nc.scalar.copy(out=dst, in_=src)
-            else:
-                nc.vector.tensor_copy(out=dst, in_=src)
+        def weave(name, rows, width, copy):
+            xb = tile("xb" + name, [P, PACK * width], BF16)
+            copy(
+                out=xb[:].rearrange("p (c i t) -> p c t i", i=4, t=PACK),
+                in_=rows[:].rearrange("p t (c i) -> p c t i", i=4),
+            )
             return xb
 
-        def quantise(name, xb, n):
-            xw = tile("xw" + name, [P, n], U32)
-            xs = tile("xs" + name, [P, n], U8)
+        def quantise(name, xb, width):
+            xw = tile("xw" + name, [P, width], U32)
+            xs = tile("xs" + name, [P, width], U8)
             nc.vector.quantize_mx(out=xw[:].bitcast(FP8X4), scales=xs[:], in_=xb[:])
             return xw, xs
 
-        HALF = NP // 2
-        rows0 = [tile("rows0%d" % u, [P, 4, NP], BF16) for u in range(2)]
-        for t in range(4):
-            both = tile("both%d" % t, [P, 2, NP], F32, tag="w1bf1" if t == 2 else None)
+        rows0 = [placed("rows0%d" % u, [P, PACK, NP], BF16, AT_TAB_SCALES + 2 * PACK * NP * u) for u in range(2)]
+        for t in range(PACK):
+            both = tile("both%d" % t, [P, 2, NP], F32, tag="w1bf1" if t == SLICES_BEFORE_W1_QUANTISE else None)
             for u in range(2):
                 pick(0, t, u, 0, NP, both[:, u, :])
                 scale(0, t, u, both[:, u, :], rows0[u])
-            if t == 1:
+            if t == SLICES_BEFORE_W1_QUANTISE - 1:
                 nc.vector.tensor_copy(v2w[1][:], tab2w1[:].bitcast(U32).indirect(idx2[:]))
 
-        pk10 = [tile("pk10%d" % t, [P, NP], F32) for t in range(4)]
-        pk110 = [tile("pk110%d" % t, [P, HALF], F32) for t in range(4)]
-        for t in range(4):
-            pick(1, t, 0, 0, NP, pk10[t][:])
-        for t in range(4):
-            pick(1, t, 1, 0, HALF, pk110[t][:])
-        x00 = quantise("00", weave("00", rows0[0], NP, True), NP)
-        pk111 = tile("pk111", [P, 4, HALF], F32, tag="xb00")
-        for t in range(4):
-            pick(1, t, 1, HALF, NP, pk111[:, t, :])
-        x01 = quantise("01", weave("01", rows0[1], NP, True), NP)
+        picked_x1 = [tile("pk10%d" % t, [P, NP], F32) for t in range(PACK)]
+        picked_x2_lo = [tile("pk110%d" % t, [P, HALF], F32) for t in range(PACK)]
+        for t in range(PACK):
+            pick(1, t, 0, 0, NP, picked_x1[t][:])
+        for t in range(PACK):
+            pick(1, t, 1, 0, HALF, picked_x2_lo[t][:])
+        x1_g0 = quantise("00", weave("00", rows0[0], NP, nc.scalar.copy), NP)
+        picked_x2_hi = tile("pk111", [P, PACK, HALF], F32, tag="xb00")
+        for t in range(PACK):
+            pick(1, t, 1, HALF, NP, picked_x2_hi[:, t, :])
+        x2_g0 = quantise("01", weave("01", rows0[1], NP, nc.scalar.copy), NP)
 
-        rows10 = tile("rows10", [P, 4, NP], BF16)
-        rows11 = [tile("rows11%d" % jh, [P, 4, HALF], BF16) for jh in range(2)]
-        for t in range(4):
-            scale(1, t, 0, pk10[t][:], rows10)
-        xb10 = weave("10", rows10, NP, False)
-        for t in range(4):
-            scale(1, t, 1, pk110[t][:], rows11[0])
-        for t in range(4):
-            scale(1, t, 1, pk111[:, t, :], rows11[1])
-        x10 = quantise("10", xb10, NP)
-        xb110 = weave("110", rows11[0], HALF, False)
-        xb111 = weave("111", rows11[1], HALF, True)
-        x110 = quantise("110", xb110, HALF)
-        x111 = quantise("111", xb111, HALF)
-        x11 = [x110, x111]
+        rows_x1 = tile("rows10", [P, PACK, NP], BF16)
+        rows_x2 = [tile("rows11%d" % jh, [P, PACK, HALF], BF16) for jh in range(2)]
+        for t in range(PACK):
+            scale(1, t, 0, picked_x1[t][:], rows_x1)
+        woven_x1 = weave("10", rows_x1, NP, nc.vector.tensor_copy)
+        for t in range(PACK):
+            scale(1, t, 1, picked_x2_lo[t][:], rows_x2[0])
+        for t in range(PACK):
+            scale(1, t, 1, picked_x2_hi[:, t, :], rows_x2[1])
+        x1_g1 = quantise("10", woven_x1, NP)
+        woven_x2_lo = weave("110", rows_x2[0], HALF, nc.vector.tensor_copy)
+        woven_x2_hi = weave("111", rows_x2[1], HALF, nc.scalar.copy)
+        x2_g1 = [quantise("110", woven_x2_lo, HALF), quantise("111", woven_x2_hi, HALF)]
 
         out_v = out.rearrange("(c p) j -> p c j", p=P)
         accs = {}
         for jh in range(2):
-            for mp in range(2):
-                accs[jh, mp] = psum.tile([P, 2, HALF], F32, name="acc2", tag="second")
-        for n, a in enumerate((0, 0, 1, 1)):
+            for pair in range(2):
+                accs[jh, pair] = psum.tile([P, 2, HALF], F32, name="acc2", tag="second")
+        for n, g in enumerate((0, 0, 1, 1)):
             for jh in range(2):
-                cols = slice(HALF * jh, HALF * (jh + 1))
-                xw, xs = (x00, x01, x10, x11[jh])[n]
-                xcols = cols if n < 3 else slice(0, HALF)
-                for c in range(4):
+                xw, xs = (x1_g0, x2_g0, x1_g1, x2_g1[jh])[n]
+                last = n == 3
+                xcols = slice(0, HALF) if last else slice(HALF * jh, HALF * (jh + 1))
+                for c in range(S2 // P):
                     nc.tensor.matmul_mx(
                         out=accs[jh, c // 2][:, c % 2, :],
-                        lhsT=v2w[a][:, P * c : P * (c + 1)].bitcast(FP8X4),
-                        lhsT_scale=v2s[4 * a : P, P * c : P * (c + 1)],
+                        lhsT=v2w[g][:, P * c : P * (c + 1)].bitcast(FP8X4),
+                        lhsT_scale=v2s[PACK * g : P, P * c : P * (c + 1)],
                         rhs=xw[:, xcols].bitcast(FP8X4),
                         rhs_scale=xs[:, xcols],
                         start=(n == 0 and c % 2 == 0),
-                        stop=(n == 3 and c % 2 == 1),
+                        stop=(last and c % 2 == 1),
                     )
         for jh in range(2):
-            cols = slice(HALF * jh, HALF * (jh + 1))
-            for mp in range(2):
-                res = tile("res%d%d" % (jh, mp), [P, 2, HALF], F32)
+            for pair in range(2):
+                res = tile("res%d%d" % (jh, pair), [P, 2, HALF], F32)
                 for e in range(2):
-                    c = 2 * mp + e
-                    if mp == 1:
-                        nc.vector.tensor_scalar(out=res[:, e, :], in0=accs[jh, mp][:, e, :], scalar1=vl[:, c : c + 1], scalar2=None, op0=ALU.mult)
+                    c = 2 * pair + e
+                    factor = veil_sb[:, c : c + 1]
+                    if pair == 1:
+                        nc.vector.tensor_scalar(out=res[:, e, :], in0=accs[jh, pair][:, e, :], scalar1=factor, scalar2=None, op0=ALU.mult)
                     else:
-                        nc.scalar.activation(out=res[:, e, :], in_=accs[jh, mp][:, e, :], func=ACT.Copy, scale=vl[:, c : c + 1])
-                nc.sync.dma_start(out=out_v[:, 2 * mp : 2 * mp + 2, cols], in_=res[:])
+                        nc.scalar.activation(out=res[:, e, :], in_=accs[jh, pair][:, e, :], func=ACT.Copy, scale=factor)
+                nc.sync.dma_start(out=out_v[:, 2 * pair : 2 * pair + 2, HALF * jh : HALF * (jh + 1)], in_=res[:])

from contextlib import ExitStack

import concourse.mybir as mybir

K, H, T, S, S2, T3, NP = 1024, 1024, 4096, 1024, 512, 2048, 512
FLOPS = 2 * K * H * S + 2 * 2 * H * S2 * NP

F32 = mybir.dt.float32
BF16 = mybir.dt.bfloat16
I32 = mybir.dt.int32
U32 = mybir.dt.uint32
U16 = mybir.dt.uint16
U8 = mybir.dt.uint8
FP8X4 = mybir.dt.float8_e4m3fn_x4
FP4X4 = mybir.dt.float4_e2m1fn_x4
ACT = mybir.ActivationFunctionType
ALU = mybir.AluOpType

P = 128
PACK = 4
PASS = P * PACK
BANK = 512
QUAD = 32
GROUP = 16
HALF = NP // 2
TAB_SCALE_LOADS_ON_GPSIMD = 2
SLICES_BEFORE_W1_QUANTISE = 2

AT_TAB_PASS0 = 0
AT_V2_SCALES = 4 * T3
AT_TAB2_SCALES = 4 * T
AT_W4_SCALES_RAW = AT_TAB2_SCALES + T3 - H // 2
AT_TAB2_PASS0 = AT_TAB2_SCALES + T3
AT_TAB_SCALES = AT_TAB2_PASS0 + 4 * T3


def tile_list_gown_veil_suggestion_kernel(
    tc, tab_words, tab_scales, offs, w1, w4_words, w4_scales, b, gain, tried,
    tab2_words, tab2_scales, offs2, pos1, pos2, veil, out,
):
    nc = tc.nc
    with ExitStack() as ctx:
        keep = ctx.enter_context(tc.tile_pool(name="keep", bufs=1))
        turns = ctx.enter_context(tc.tile_pool(name="turns", bufs=1))
        psum = ctx.enter_context(tc.psum_pool(name="psum", bufs=4))

        def tile(name, shape, dtype, tag=None):
            return keep.tile(shape, dtype, name=name, tag=tag or name, align_bytes=64)

        def placed(name, shape, dtype, offset):
            return turns.tile(shape, dtype, name=name, align_bytes=64, offset=offset)

        def words_of(table, a):
            return table[a].rearrange("p t i -> p (t i)").bitcast(I32)

        idx = tile("idx", [P, S // GROUP], U16)
        idx2 = tile("idx2", [P, S2 // GROUP], U16)
        p1 = tile("p1", [P, NP // GROUP], U16)
        p2 = tile("p2", [P, NP // GROUP], U16)
        tabw1 = tile("tabw1", [P, T], I32)
        tabs = placed("tabs", [P, T], U8, AT_TAB_SCALES)
        w4raw = tile("w4raw", [P, 2 * H], U8)
        w4sraw = placed("w4sraw", [P, H], U8, AT_W4_SCALES_RAW)
        w1raw0 = placed("w1raw0", [P, PACK, PASS], F32, AT_TAB_PASS0)

        nc.vector.memset(w4sraw[:].bitcast(I32), 0)
        nc.vector.memset(tabs[:].bitcast(I32), 0)

        def load_w1(g, raw):
            nc.sync.dma_start(out=raw[:], in_=w1[:, PASS * g : PASS * (g + 1)].rearrange("(p i) c -> p i c", i=PACK))

        def load_scale_rows(queue, plane, first, scales, r):
            queue.dma_start(out=plane[first + r : P : QUAD, :].bitcast(I32), in_=scales[r : PACK * PACK : PACK, :].bitcast(I32))

        nc.sync.dma_start(out=w4raw[:].bitcast(I32), in_=w4_words[0].bitcast(I32))
        nc.sync.dma_start(idx[:], offs)
        nc.sync.dma_start(p1[:], pos1)
        nc.sync.dma_start(p2[:], pos2)
        nc.sync.dma_start(idx2[:], offs2)
        load_w1(0, w1raw0)
        for r in range(PACK):
            load_scale_rows(nc.sync, w4sraw, 0, w4_scales[0], r)
        nc.sync.dma_start(out=tabw1[:], in_=words_of(tab_words, 1))
        for n in range(2 * PACK):
            a, r = n % 2, n // 2
            queue = nc.gpsimd if n < TAB_SCALE_LOADS_ON_GPSIMD else nc.sync
            load_scale_rows(queue, tabs, PACK * (1 - a), tab_scales[a], r)

        w4w = tile("w4w", [P, 2 * H], U8)
        nc.vector.tensor_copy(
            out=w4w[:].bitcast(U16).rearrange("p (g t m) -> p g t m", g=2, t=PACK),
            in_=w4raw[:].bitcast(U16).rearrange("p (g m t) -> p g t m", g=2, t=PACK),
        )

        consts = tile("consts", [P, 4, 8], F32, tag="w4raw")
        bias, gain_sb, tried_sb, veil_sb = (consts[:, n, :] for n in range(4))
        for vec, dst in ((b, bias), (gain, gain_sb), (tried, tried_sb)):
            nc.gpsimd.dma_start(out=dst.rearrange("p (g t) -> p g t", g=2), in_=vec.rearrange("(g p t) -> p g t", g=2, t=PACK))
        with nc.allow_non_contiguous_dma(reason="one value of veil for each partition"):
            nc.gpsimd.dma_start(out=veil_sb[:, 0 : S2 // P], in_=veil.rearrange("(c p) -> p c", p=P))
        gain_tried = tile("gt", [P, 8], F32)
        nc.gpsimd.tensor_tensor(gain_tried[:], gain_sb, tried_sb, ALU.mult)

        w1w = [tile("w1w%d" % g, [P, PASS], U32) for g in range(2)]
        w1s = [tile("w1s%d" % g, [P, PASS], U8) for g in range(2)]

        def weave_w1(g, raw, copy):
            wb = tile("w1bf%d" % g, [P, PACK * PASS], BF16)
            copy(
                out=wb[:].rearrange("p (t m i) -> p m t i", t=PACK, i=PACK),
                in_=raw[:].rearrange("p i (m t) -> p m t i", t=PACK),
            )
            return wb

        def quantise_w1(g, wb):
            nc.vector.quantize_mx(out=w1w[g][:].bitcast(FP8X4), scales=w1s[g][:], in_=wb[:])

        wb0 = weave_w1(0, w1raw0, nc.vector.tensor_copy)
        tabw0 = placed("tabw0", [P, T], I32, AT_TAB_PASS0)
        nc.sync.dma_start(out=tabw0[:], in_=words_of(tab_words, 0))
        quantise_w1(0, wb0)
        w4s = tile("w4s", [P, H], U8, tag="w1bf0")
        nc.vector.tensor_copy(
            out=w4s[:].rearrange("p (g t m) -> p g t m", g=2, t=PACK),
            in_=w4sraw[:].rearrange("p (g m t) -> p g t m", g=2, t=PACK),
        )

        tab2s = placed("tab2s", [P, T3], U8, AT_TAB2_SCALES)
        nc.vector.memset(tab2s[:].bitcast(I32), 0)
        for q in range(P // QUAD):
            nc.sync.dma_start(
                out=tab2s[QUAD * q : QUAD * q + 2 * PACK, :].bitcast(I32),
                in_=tab2_scales[:, PACK * q : PACK * (q + 1), :].bitcast(I32),
            )
        tab2w0 = placed("tab2w0", [P, T3], I32, AT_TAB2_PASS0)
        nc.sync.dma_start(out=tab2w0[:], in_=words_of(tab2_words, 0))

        vw = [tile("vw%d" % a, [P, S], U32) for a in range(2)]
        vs = tile("vs", [P, S], U8)
        nc.vector.tensor_copy(vw[1][:], tabw1[:].bitcast(U32).indirect(idx[:]))
        nc.vector.tensor_copy(vs[:], tabs[:].indirect(idx[:]))
        w1raw1 = placed("w1raw1", [P, PACK, PASS], F32, AT_TAB_SCALES)
        load_w1(1, w1raw1)
        for half in range(2):
            nc.vector.tensor_copy(
                vw[0][:, BANK * half : BANK * (half + 1)],
                tabw0[:].bitcast(U32).indirect(idx[:, BANK // GROUP * half : BANK // GROUP * (half + 1)]),
            )
        tab2w1 = placed("tab2w1", [P, T3], I32, AT_TAB_PASS0)
        nc.sync.dma_start(out=tab2w1[:], in_=words_of(tab2_words, 1))

        v2w = [tile("v2w%d" % a, [P, S2], U32) for a in range(2)]
        v2s = placed("v2s", [P, S2], U8, AT_V2_SCALES)
        nc.vector.tensor_copy(v2s[:], tab2s[:].indirect(idx2[:]))
        nc.vector.tensor_copy(v2w[0][:], tab2w0[:].bitcast(U32).indirect(idx2[:]))

        slices = {}

        def first_product(g):
            for t in range(PACK):
                act = tile("h%d%d" % (g, t), [P, S], F32)
                slices[g, t] = act
                c0 = PASS * g + P * t
                banks = [psum.tile([P, BANK], F32, name="acc", tag="first") for half in range(2)]
                for half in range(2):
                    cols = slice(BANK * half, BANK * (half + 1))
                    nc.tensor.matmul_mx(
                        out=banks[half][:],
                        lhsT=w4w[:, 2 * c0 : 2 * (c0 + P)].bitcast(FP4X4),
                        lhsT_scale=w4s[:, c0 : c0 + P],
                        rhs=vw[1][:, cols].bitcast(FP8X4),
                        rhs_scale=vs[:, cols],
                        start=True,
                        stop=False,
                    )
                for half in range(2):
                    cols = slice(BANK * half, BANK * (half + 1))
                    nc.tensor.matmul_mx(
                        out=banks[half][:],
                        lhsT=w1w[g][:, P * t : P * (t + 1)].bitcast(FP8X4),
                        lhsT_scale=w1s[g][:, P * t : P * (t + 1)],
                        rhs=vw[0][:, cols].bitcast(FP8X4),
                        rhs_scale=vs[PACK:P, cols],
                        start=False,
                        stop=True,
                    )
                    n = PACK * g + t
                    nc.scalar.activation(out=act[:, cols], in_=banks[half][:], func=ACT.Silu, bias=bias[:, n : n + 1])

        first_product(0)
        quantise_w1(1, weave_w1(1, w1raw1, nc.scalar.copy))
        first_product(1)

        lists = (p1, p2)
        factors = (gain_tried, gain_sb)

        def pick(g, t, u, j0, j1, picked):
            nc.vector.tensor_copy(picked, slices[g, t][:].indirect(lists[u][:, j0 // GROUP : j1 // GROUP]))

        def scale(g, t, u, picked, rows):
            n = PACK * g + t
            nc.scalar.activation(out=rows[:, t, :], in_=picked, func=ACT.Copy, scale=factors[u][:, n : n + 1])

        def weave(name, rows, width, copy):
            xb = tile("xb" + name, [P, PACK * width], BF16)
            copy(
                out=xb[:].rearrange("p (c i t) -> p c t i", i=4, t=PACK),
                in_=rows[:].rearrange("p t (c i) -> p c t i", i=4),
            )
            return xb

        def quantise(name, xb, width):
            xw = tile("xw" + name, [P, width], U32)
            xs = tile("xs" + name, [P, width], U8)
            nc.vector.quantize_mx(out=xw[:].bitcast(FP8X4), scales=xs[:], in_=xb[:])
            return xw, xs

        rows0 = [placed("rows0%d" % u, [P, PACK, NP], BF16, AT_TAB_SCALES + 2 * PACK * NP * u) for u in range(2)]
        for t in range(PACK):
            both = tile("both%d" % t, [P, 2, NP], F32, tag="w1bf1" if t == SLICES_BEFORE_W1_QUANTISE else None)
            for u in range(2):
                pick(0, t, u, 0, NP, both[:, u, :])
                scale(0, t, u, both[:, u, :], rows0[u])
            if t == SLICES_BEFORE_W1_QUANTISE - 1:
                nc.vector.tensor_copy(v2w[1][:], tab2w1[:].bitcast(U32).indirect(idx2[:]))

        picked_x1 = [tile("pk10%d" % t, [P, NP], F32) for t in range(PACK)]
        picked_x2_lo = [tile("pk110%d" % t, [P, HALF], F32) for t in range(PACK)]
        for t in range(PACK):
            pick(1, t, 0, 0, NP, picked_x1[t][:])
        for t in range(PACK):
            pick(1, t, 1, 0, HALF, picked_x2_lo[t][:])
        x1_g0 = quantise("00", weave("00", rows0[0], NP, nc.scalar.copy), NP)
        picked_x2_hi = tile("pk111", [P, PACK, HALF], F32, tag="xb00")
        for t in range(PACK):
            pick(1, t, 1, HALF, NP, picked_x2_hi[:, t, :])
        x2_g0 = quantise("01", weave("01", rows0[1], NP, nc.scalar.copy), NP)

        rows_x1 = tile("rows10", [P, PACK, NP], BF16)
        rows_x2 = [tile("rows11%d" % jh, [P, PACK, HALF], BF16) for jh in range(2)]
        for t in range(PACK):
            scale(1, t, 0, picked_x1[t][:], rows_x1)
        woven_x1 = weave("10", rows_x1, NP, nc.vector.tensor_copy)
        for t in range(PACK):
            scale(1, t, 1, picked_x2_lo[t][:], rows_x2[0])
        for t in range(PACK):
            scale(1, t, 1, picked_x2_hi[:, t, :], rows_x2[1])
        x1_g1 = quantise("10", woven_x1, NP)
        woven_x2_lo = weave("110", rows_x2[0], HALF, nc.vector.tensor_copy)
        woven_x2_hi = weave("111", rows_x2[1], HALF, nc.scalar.copy)
        x2_g1 = [quantise("110", woven_x2_lo, HALF), quantise("111", woven_x2_hi, HALF)]

        out_v = out.rearrange("(c p) j -> p c j", p=P)
        accs = {}
        for jh in range(2):
            for pair in range(2):
                accs[jh, pair] = psum.tile([P, 2, HALF], F32, name="acc2", tag="second")
        for n, g in enumerate((0, 0, 1, 1)):
            for jh in range(2):
                xw, xs = (x1_g0, x2_g0, x1_g1, x2_g1[jh])[n]
                last = n == 3
                xcols = slice(0, HALF) if last else slice(HALF * jh, HALF * (jh + 1))
                for c in range(S2 // P):
                    nc.tensor.matmul_mx(
                        out=accs[jh, c // 2][:, c % 2, :],
                        lhsT=v2w[g][:, P * c : P * (c + 1)].bitcast(FP8X4),
                        lhsT_scale=v2s[PACK * g : P, P * c : P * (c + 1)],
                        rhs=xw[:, xcols].bitcast(FP8X4),
                        rhs_scale=xs[:, xcols],
                        start=(n == 0 and c % 2 == 0),
                        stop=(last and c % 2 == 1),
                    )
        for jh in range(2):
            for pair in range(2):
                res = tile("res%d%d" % (jh, pair), [P, 2, HALF], F32)
                for e in range(2):
                    c = 2 * pair + e
                    factor = veil_sb[:, c : c + 1]
                    if pair == 1:
                        nc.vector.tensor_scalar(out=res[:, e, :], in0=accs[jh, pair][:, e, :], scalar1=factor, scalar2=None, op0=ALU.mult)
                    else:
                        nc.scalar.activation(out=res[:, e, :], in_=accs[jh, pair][:, e, :], func=ACT.Copy, scale=factor)
                nc.sync.dma_start(out=out_v[:, 2 * pair : 2 * pair + 2, HALF * jh : HALF * (jh + 1)], in_=res[:])
